import numpy as np
import ml_dtypes


def mxq(x, axis, fmt="e4m3"):
    dtype, down = {"e4m3": (ml_dtypes.float8_e4m3fn, 7), "e5m2": (ml_dtypes.float8_e5m2, 14)}[fmt]
    v = np.moveaxis(np.asarray(x, np.float32).astype(ml_dtypes.bfloat16).astype(np.float64), axis, -1)
    blocks = v.reshape(v.shape[:-1] + (-1, 32))
    amax = np.abs(blocks).max(-1, keepdims=True)
    byte = np.maximum(np.where(amax > 0, np.frexp(amax)[1] - 1 + 127, 0) - down, 1)
    scale = np.exp2(byte - 127.0)
    codes = (blocks / scale).astype(np.float32).astype(dtype).astype(np.float64)
    return np.moveaxis((codes * scale).reshape(v.shape), -1, axis)


WIDE = False


def mx_kscale(k):
    if not WIDE:
        return np.ones(k)
    levels = np.array([10, -10, 5, -5, 0])
    if k % 512:
        return np.exp2(np.random.permutation(np.resize(levels, k // 32))).repeat(32)
    a = np.empty((k // 512, 16))
    for p in range(k // 512):
        a[p, :8] = np.random.permutation(np.resize(levels, 8))
        for g in range(8):
            far = levels[np.abs(levels - a[p, g]) >= 10]
            a[p, g + 8] = far[np.random.randint(len(far))]
    return np.exp2(a.ravel()).repeat(32)


def f64(x):
    return np.asarray(x).astype(np.float64)


def striped(idx):
    return np.tile(idx.reshape(-1, 16).T, (8, 1)).astype(np.uint16)


def unstriped(offs):
    return offs[:16].T.reshape(-1).astype(np.int64)


E2M1 = np.array([0.0, 0.5, 1.0, 1.5, 2.0, 3.0, 4.0, 6.0, -0.0, -0.5, -1.0, -1.5, -2.0, -3.0, -4.0, -6.0])


def pack_weight(w, fmt):
    k, n = w.shape
    w = f64(np.asarray(w, np.float32).astype(ml_dtypes.bfloat16)).reshape(k // 32, 32, n)
    amax = np.abs(w).max(1)
    if fmt == "e4m3":
        byte = np.frexp(amax)[1] - 1 + 127 - 7
    else:
        mant, ex = np.frexp(amax / 6.0)
        byte = np.where(mant > 0.5, ex, ex - 1) + 127
    byte = np.clip(np.where(amax > 0, byte, 1), 1, 254)
    scaled = (w * np.exp2(127.0 - byte)[:, None, :]).reshape(k, n).astype(np.float32)
    by_word = np.ascontiguousarray(scaled.reshape(k // 512, 128, 4, n).transpose(0, 1, 3, 2))
    if fmt == "e4m3":
        words = by_word.astype(ml_dtypes.float8_e4m3fn).view(np.uint8)
    else:
        c = by_word.astype(ml_dtypes.float4_e2m1fn).view(np.uint8) & 0xF
        words = (c[..., 0::2] | (c[..., 1::2] << 4)).reshape(k // 512, 128, 2 * n)
    return np.ascontiguousarray(words), np.ascontiguousarray(byte.astype(np.uint8).reshape(k // 512, 16, n))


def unpack_weight(words, scales, fmt):
    g, _, n = scales.shape
    words = np.ascontiguousarray(words).reshape(g, 128, n, -1)
    if fmt == "e4m3":
        vals = words.view(ml_dtypes.float8_e4m3fn).astype(np.float64)
    else:
        nib = np.empty((g, 128, n, 4), np.uint8)
        nib[..., 0::2] = words & 0xF
        nib[..., 1::2] = words >> 4
        vals = E2M1[nib]
    vals = vals * np.repeat(np.exp2(scales.astype(np.float64) - 127.0), 8, axis=1)[..., None]
    return vals.transpose(0, 1, 3, 2).reshape(g * 512, n)


def relu2(v):
    return np.maximum(v, 0.0) ** 2


K, T, E, C, N = 1536, 768, 18, 128, 128
TOP = 3


def by_expert(wq, xq):
    return np.concatenate([wq[e].T @ xq[:, e * C:(e + 1) * C] for e in range(E)], axis=1)


def setup_inputs():
    n = np.random.standard_normal
    s = mx_kscale(K)[:, None]
    deal = np.repeat(np.arange(E), C).reshape(TOP, T)[:, np.random.permutation(T)]
    deal = np.take_along_axis(deal, np.argsort(np.random.rand(TOP, T), axis=0), axis=0)
    for _ in range(8):
        s_, t_ = np.random.permutation(T).reshape(2, -1); r = np.random.randint(TOP, size=T // 2); x, y = deal[r, s_].copy(), deal[r, t_].copy()
        ok = ~((deal[:, s_] == y).any(0) | (deal[:, t_] == x).any(0)); deal[r[ok], s_[ok]] = y[ok]; deal[r[ok], t_[ok]] = x[ok]
    order = np.lexsort((np.random.rand(TOP * T), deal.reshape(-1)))
    slot_token = order % T; pos = np.empty(TOP * T, np.int64); pos[order] = np.arange(TOP * T); pos = pos.reshape(TOP, T)
    g = np.random.uniform(0.5, 1.5, (TOP, T)); g = g / g.sum(0)
    w = [pack_weight(m, "e2m1") for m in n((E + 1, K, N)) / np.sqrt(K) / s[None]]
    return {
        "xT": (n((K, T)) * s).astype(np.float32),
        "w_words": np.stack([m[0] for m in w]),
        "w_scales": np.stack([m[1] for m in w]),
        "b": (0.3 * n((N, E + 1))).astype(np.float32),
        "gate": np.stack([np.tile(r, (N, 1)) for r in g]).astype(np.float32),
        "offs": striped(slot_token),
        "pos1": striped(pos[0]),
        "pos2": striped(pos[1]),
        "pos3": striped(pos[2]),
    }


def reference(xT, w_words, w_scales, b, gate, offs, pos1, pos2, pos3):
    idx = unstriped(offs)
    w = np.stack([unpack_weight(w_words[e], w_scales[e], "e2m1") for e in range(E + 1)])
    wq = w
    xs = mxq(f64(xT), 0, "e4m3")
    ys = relu2((wq[E].T @ xs) + f64(b)[:, E:])
    xq = mxq(f64(xT)[:, idx], 0, "e4m3")
    y = by_expert(w, xq)
    y = relu2(y + np.repeat(f64(b)[:, :E], C, axis=1))
    return ys + sum(f64(gate[r]) * y[:, unstriped(p)] for r, p in enumerate((pos1, pos2, pos3)))

@@ -1,0 +1,219 @@
+from contextlib import ExitStack
+
+import concourse.mybir as mybir
+
+K, T, E, C, N = 1536, 768, 18, 128, 128
+S = E * C
+P = 128
+PASSES = K // 512
+FLOPS = 2 * K * N * (S + T)
+
+F32 = mybir.dt.float32
+BF16 = mybir.dt.bfloat16
+I32 = mybir.dt.int32
+U32 = mybir.dt.uint32
+U16 = mybir.dt.uint16
+U8 = mybir.dt.uint8
+FP8X4 = mybir.dt.float8_e4m3fn_x4
+FP4X4 = mybir.dt.float4_e2m1fn_x4
+ACT = mybir.ActivationFunctionType
+ALU = mybir.AluOpType
+
+CHUNKS = [512, 512, 512, 512, 256]
+LAST_CHUNKS = [512, 512, 512, 256, 256, 128, 128]
+TOKEN_PARTS = [(0, 512), (512, 256)]
+
+
+def spans(widths):
+    out, start = [], 0
+    for w in widths:
+        out.append((start, w))
+        start += w
+    return out
+
+
+def tile_moe_shr_lin_relu2_kernel(
+    tc, xT, w_words, w_scales, b, gate, offs, pos1, pos2, pos3, out
+):
+    nc = tc.nc
+    with ExitStack() as ctx:
+        keep = ctx.enter_context(tc.tile_pool(name="keep", bufs=1))
+        ring = ctx.enter_context(tc.tile_pool(name="ring", bufs=4))
+        psum = ctx.enter_context(tc.psum_pool(name="psum", bufs=1))
+
+        offs_sb = keep.tile([P, S // 16], U16, name="offs_sb")
+        pos_sb = [keep.tile([P, T // 16], U16, name=f"pos_sb{r}") for r in range(3)]
+        raw = [[keep.tile([P, 2, T], F32, name=f"raw{a}{u}") for u in range(2)] for a in range(PASSES)]
+        pairs = [keep.tile([P, 2, T], U32, name=f"pairs{a}", align_bytes=64) for a in range(PASSES)]
+        w_sb = keep.tile([P, (E + 1) * PASSES, 2 * N], U8, name="w_sb", align_bytes=64)
+        ws_sb = keep.tile([P, (E + 1) * PASSES, N], U8, name="ws_sb", align_bytes=64)
+        b_sb = keep.tile([P, E + 1], F32, name="b_sb")
+        gate_sb = keep.tile([P, 3, T], F32, name="gate_sb")
+        codes = [keep.tile([P, S], U32, name=f"codes{a}", align_bytes=64) for a in range(PASSES)]
+        scales = [keep.tile([P, S], U8, name=f"scales{a}", align_bytes=64) for a in range(PASSES)]
+        sh_quads = [keep.tile([P, T, 2], U32, name=f"sh_quads{a}", align_bytes=64) for a in range(PASSES)]
+        sh_codes = [keep.tile([P, T], U32, name=f"sh_codes{a}", align_bytes=64) for a in range(PASSES)]
+        sh_scales = [keep.tile([P, T], U8, name=f"sh_scales{a}", align_bytes=64) for a in range(PASSES)]
+        y = keep.tile([P, S], F32, name="y")
+        ys = keep.tile([P, T], F32, name="ys")
+        warm = keep.tile([P, 2], F32, name="warm")
+
+        nc.vector.memset(warm[:, 0:1], 0.0)
+        nc.scalar.activation(warm[:, 1:2], warm[:, 0:1], ACT.Relu)
+        nc.vector.memset(ws_sb[:].rearrange("p g n -> p (g n)").bitcast(I32), 0)
+
+        def x_rows(a, u):
+            return xT[512 * a : 512 * (a + 1), :].rearrange("(p j) t -> p j t", j=4)[:, 2 * u : 2 * u + 2, :]
+
+        H = T // 2
+        for h in range(2):
+            nc.sync.dma_start(out=raw[0][0][:, :, h * H : (h + 1) * H], in_=x_rows(0, 0)[:, :, h * H : (h + 1) * H])
+        nc.sync.dma_start(offs_sb[:], offs)
+        for a in range(PASSES):
+            for u in range(2):
+                if (a, u) != (0, 0):
+                    nc.sync.dma_start(out=raw[a][u][:], in_=x_rows(a, u))
+        scale_rows = w_scales.rearrange("e a q n -> q (e a) n").bitcast(I32)
+        for q in range(4):
+            nc.sync.dma_start(out=ws_sb[32 * q : 32 * q + 4, :, :].bitcast(I32), in_=scale_rows[4 * q : 4 * q + 4])
+        nc.sync.dma_start(out=b_sb[:], in_=b)
+        word_rows = w_words.rearrange("e a p c -> p (e a) c").bitcast(I32)
+        for g0, g1 in ((0, 18), (18, 36), (36, 57)):
+            nc.sync.dma_start(out=w_sb[:, g0:g1, :].bitcast(I32), in_=word_rows[:, g0:g1, :])
+        for r, pos in enumerate((pos1, pos2, pos3)):
+            nc.sync.dma_start(pos_sb[r][:], pos)
+        nc.sync.dma_start(out=gate_sb[:], in_=gate.rearrange("r p t -> p r t"))
+
+        def cast(engine_copy, a, u, t0, t1):
+            dst = pairs[a][:, u, t0:t1].bitcast(BF16).rearrange("p (t j) -> p t j", j=2)
+            engine_copy(dst, raw[a][u][:, :, t0:t1].rearrange("p j t -> p t j"))
+
+        def interleave(dst, src):
+            nc.scalar.copy(dst.bitcast(F32), src.bitcast(F32).rearrange("p u s -> p s u"))
+
+        def quantize(dst_codes, dst_scales, quads):
+            nc.vector.quantize_mx(
+                out=dst_codes.bitcast(FP8X4),
+                scales=dst_scales,
+                in_=quads.rearrange("p s u -> p (s u)").bitcast(BF16),
+            )
+
+        def product(acc, e, rhs_codes, rhs_scales, cols):
+            for a in range(PASSES):
+                g = e * PASSES + a
+                nc.tensor.matmul_mx(
+                    out=acc,
+                    lhsT=w_sb[:, g, :].bitcast(FP4X4),
+                    lhsT_scale=ws_sb[:, g, :],
+                    rhs=rhs_codes[a][:, cols].bitcast(FP8X4),
+                    rhs_scale=rhs_scales[a][:, cols],
+                    start=(a == 0),
+                    stop=(a == PASSES - 1),
+                )
+
+        steps = []
+        for a in range(PASSES):
+            for s0, w in spans(LAST_CHUNKS if a == PASSES - 1 else CHUNKS):
+                steps.append((a, s0, w))
+        planes, quads = {}, {}
+
+        def gather(i, u):
+            a, s0, w = steps[i]
+            if i not in planes:
+                planes[i] = ring.tile([P, 2, w], U32, name="planes", align_bytes=64)
+            nc.vector.tensor_copy(
+                planes[i][:, u, :], pairs[a][:, u, :].indirect(offs_sb[:, s0 // 16 : (s0 + w) // 16])
+            )
+
+        def weave(i):
+            w = steps[i][2]
+            quads[i] = ring.tile([P, w, 2], U32, name="quads", align_bytes=64)
+            interleave(quads[i][:], planes[i][:])
+
+        def finish(i):
+            a, s0, w = steps[i]
+            quantize(codes[a][:, s0 : s0 + w], scales[a][:, s0 : s0 + w], quads[i][:])
+            if a == PASSES - 1:
+                relu = ring.tile([P, w], F32, name="relu")
+                for c0 in range(0, w, C):
+                    e = (s0 + c0) // C
+                    acc = psum.tile([P, C], F32, name="acc", bufs=6)
+                    product(acc[:], e, codes, scales, slice(s0 + c0, s0 + c0 + C))
+                    nc.scalar.activation(relu[:, c0 : c0 + C], acc[:], ACT.Relu, bias=b_sb[:, e : e + 1])
+                nc.scalar.activation(y[:, s0 : s0 + w], relu[:], ACT.Square)
+
+        side = {
+            0: [lambda: cast(nc.scalar.copy, 1, 0, 0, T)],
+            1: [lambda: cast(nc.scalar.copy, 1, 1, 0, T)],
+            3: [lambda: interleave(sh_quads[0][:], pairs[0][:])],
+            5: [lambda: cast(nc.scalar.copy, 2, 0, 0, T)],
+            6: [lambda: cast(nc.scalar.copy, 2, 1, 0, T)],
+            7: [lambda: interleave(sh_quads[1][:], pairs[1][:])],
+            8: [lambda: interleave(sh_quads[2][:], pairs[2][:])],
+        }
+
+        cast(nc.vector.tensor_copy, 0, 0, 0, H)
+        cast(nc.vector.tensor_copy, 0, 0, H, T)
+        cast(nc.scalar.copy, 0, 1, 0, T)
+        for i in range(3):
+            gather(i, 0)
+        for i in range(len(steps)):
+            if i >= 3:
+                gather(i, 0)
+            if i >= 2:
+                finish(i - 2)
+            gather(i, 1)
+            weave(i)
+            for work in side.get(i, []):
+                work()
+        last = len(steps) - 1
+        finish(last - 1)
+        t0, w = TOKEN_PARTS[0]
+        quantize(sh_codes[0][:, t0 : t0 + w], sh_scales[0][:, t0 : t0 + w], sh_quads[0][:, t0 : t0 + w, :])
+        finish(last)
+        for part, (t0, w) in enumerate(TOKEN_PARTS):
+            for a in range(PASSES):
+                if (part, a) != (0, 0):
+                    quantize(sh_codes[a][:, t0 : t0 + w], sh_scales[a][:, t0 : t0 + w], sh_quads[a][:, t0 : t0 + w, :])
+            acc = psum.tile([P, w], F32, name=f"sh_acc{part}")
+            n = w if w == 512 else C
+            for c0 in range(0, w, n):
+                product(acc[:, c0 : c0 + n], E, sh_codes, sh_scales, slice(t0 + c0, t0 + c0 + n))
+            relu = ring.tile([P, w], F32, name="relu")
+            nc.scalar.activation(relu[:], acc[:], ACT.Relu, bias=b_sb[:, E : E + 1])
+            nc.scalar.activation(ys[:, t0 : t0 + w], relu[:], ACT.Square)
+
+        terms = keep.tile([P, 3, T], F32, name="terms")
+        sums = keep.tile([P, 3, T], F32, name="sums")
+
+        def fetch(r, part):
+            t0, w = TOKEN_PARTS[part]
+            nc.vector.tensor_tensor(
+                terms[:, r, t0 : t0 + w],
+                y[:].indirect(pos_sb[r][:, t0 // 16 : (t0 + w) // 16]),
+                gate_sb[:, r, t0 : t0 + w],
+                ALU.mult,
+            )
+
+        def add(part, dst, in0, in1):
+            t0, w = TOKEN_PARTS[part]
+            nc.vector.tensor_tensor(dst[:, t0 : t0 + w], in0[:, t0 : t0 + w], in1[:, t0 : t0 + w], ALU.add)
+
+        def store(part):
+            t0, w = TOKEN_PARTS[part]
+            nc.sync.dma_start(out=out[:, t0 : t0 + w], in_=sums[:, 2, t0 : t0 + w])
+
+        fetch(0, 0)
+        fetch(1, 0)
+        fetch(2, 0)
+        add(0, sums[:, 0, :], terms[:, 0, :], terms[:, 1, :])
+        fetch(0, 1)
+        add(0, sums[:, 1, :], terms[:, 2, :], ys[:])
+        fetch(1, 1)
+        add(0, sums[:, 2, :], sums[:, 0, :], sums[:, 1, :])
+        store(0)
+        fetch(2, 1)
+        add(1, sums[:, 0, :], terms[:, 0, :], terms[:, 1, :])
+        add(1, sums[:, 1, :], terms[:, 2, :], ys[:])
+        add(1, sums[:, 2, :], sums[:, 0, :], sums[:, 1, :])
+        store(1)

@@ -19,17 +19,15 @@ FP4X4 = mybir.dt.float4_e2m1fn_x4
 ACT = mybir.ActivationFunctionType
 ALU = mybir.AluOpType
 
-CHUNKS = [512, 512, 512, 512, 256]
-LAST_CHUNKS = [512, 512, 512, 256, 256, 128, 128]
+STEPS = [
+    (0, 0, 512), (0, 512, 512), (0, 1024, 512), (0, 1536, 512),
+    (1, 0, 512), (1, 512, 512), (0, 2048, 256), (2, 0, 512),
+    (1, 1024, 512), (2, 512, 512), (1, 1536, 512), (2, 1024, 512),
+    (1, 2048, 256), (2, 1536, 256), (2, 1792, 256), (2, 2048, 128), (2, 2176, 128),
+]
+BANKS = 6
+HEAD = [(0, 512), (512, 768)]
 TOKEN_PARTS = [(0, 512), (512, 256)]
-
-
-def spans(widths):
-    out, start = [], 0
-    for w in widths:
-        out.append((start, w))
-        start += w
-    return out
 
 
 def tile_moe_shr_lin_relu2_kernel(
@@ -38,7 +36,7 @@ def tile_moe_shr_lin_relu2_kernel(
     nc = tc.nc
     with ExitStack() as ctx:
         keep = ctx.enter_context(tc.tile_pool(name="keep", bufs=1))
-        ring = ctx.enter_context(tc.tile_pool(name="ring", bufs=4))
+        ring = ctx.enter_context(tc.tile_pool(name="ring", bufs=1))
         psum = ctx.enter_context(tc.psum_pool(name="psum", bufs=1))
 
         offs_sb = keep.tile([P, S // 16], U16, name="offs_sb")
@@ -52,22 +50,20 @@ def tile_moe_shr_lin_relu2_kernel(
         codes = [keep.tile([P, S], U32, name=f"codes{a}", align_bytes=64) for a in range(PASSES)]
         scales = [keep.tile([P, S], U8, name=f"scales{a}", align_bytes=64) for a in range(PASSES)]
         sh_quads = [keep.tile([P, T, 2], U32, name=f"sh_quads{a}", align_bytes=64) for a in range(PASSES)]
-        sh_codes = [keep.tile([P, T], U32, name=f"sh_codes{a}", align_bytes=64) for a in range(PASSES)]
         sh_scales = [keep.tile([P, T], U8, name=f"sh_scales{a}", align_bytes=64) for a in range(PASSES)]
         y = keep.tile([P, S], F32, name="y")
         ys = keep.tile([P, T], F32, name="ys")
         warm = keep.tile([P, 2], F32, name="warm")
 
-        nc.vector.memset(warm[:, 0:1], 0.0)
+        nc.gpsimd.memset(warm[:, 0:1], 0.0)
         nc.scalar.activation(warm[:, 1:2], warm[:, 0:1], ACT.Relu)
-        nc.vector.memset(ws_sb[:].rearrange("p g n -> p (g n)").bitcast(I32), 0)
+        nc.gpsimd.memset(ws_sb[:].rearrange("p g n -> p (g n)").bitcast(I32), 0)
 
         def x_rows(a, u):
             return xT[512 * a : 512 * (a + 1), :].rearrange("(p j) t -> p j t", j=4)[:, 2 * u : 2 * u + 2, :]
 
-        H = T // 2
-        for h in range(2):
-            nc.sync.dma_start(out=raw[0][0][:, :, h * H : (h + 1) * H], in_=x_rows(0, 0)[:, :, h * H : (h + 1) * H])
+        for t0, t1 in HEAD:
+            nc.sync.dma_start(out=raw[0][0][:, :, t0:t1], in_=x_rows(0, 0)[:, :, t0:t1])
         nc.sync.dma_start(offs_sb[:], offs)
         for a in range(PASSES):
             for u in range(2):
@@ -78,7 +74,7 @@ def tile_moe_shr_lin_relu2_kernel(
             nc.sync.dma_start(out=ws_sb[32 * q : 32 * q + 4, :, :].bitcast(I32), in_=scale_rows[4 * q : 4 * q + 4])
         nc.sync.dma_start(out=b_sb[:], in_=b)
         word_rows = w_words.rearrange("e a p c -> p (e a) c").bitcast(I32)
-        for g0, g1 in ((0, 18), (18, 36), (36, 57)):
+        for g0, g1 in ((0, 12), (12, 24), (24, 36), (36, 57)):
             nc.sync.dma_start(out=w_sb[:, g0:g1, :].bitcast(I32), in_=word_rows[:, g0:g1, :])
         for r, pos in enumerate((pos1, pos2, pos3)):
             nc.sync.dma_start(pos_sb[r][:], pos)
@@ -98,8 +94,8 @@ def tile_moe_shr_lin_relu2_kernel(
                 in_=quads.rearrange("p s u -> p (s u)").bitcast(BF16),
             )
 
-        def product(acc, e, rhs_codes, rhs_scales, cols):
-            for a in range(PASSES):
+        def product(acc, e, rhs_codes, rhs_scales, cols, passes):
+            for a in passes:
                 g = e * PASSES + a
                 nc.tensor.matmul_mx(
                     out=acc,
@@ -111,63 +107,75 @@ def tile_moe_shr_lin_relu2_kernel(
                     stop=(a == PASSES - 1),
                 )
 
-        steps = []
-        for a in range(PASSES):
-            for s0, w in spans(LAST_CHUNKS if a == PASSES - 1 else CHUNKS):
-                steps.append((a, s0, w))
+        steps = STEPS
         planes, quads = {}, {}
+        accs, ready, closed = [], [0], [0]
+
+        last = len(steps) - 1
+
+        def plane_tag(i):
+            return f"p{i % 3}"
 
         def gather(i, u):
             a, s0, w = steps[i]
             if i not in planes:
-                planes[i] = ring.tile([P, 2, w], U32, name="planes", align_bytes=64)
+                planes[i] = ring.tile([P, 2, w], U32, name=f"planes{i}", tag=plane_tag(i), align_bytes=64)
             nc.vector.tensor_copy(
                 planes[i][:, u, :], pairs[a][:, u, :].indirect(offs_sb[:, s0 // 16 : (s0 + w) // 16])
             )
 
         def weave(i):
             w = steps[i][2]
-            quads[i] = ring.tile([P, w, 2], U32, name="quads", align_bytes=64)
+            quads[i] = ring.tile([P, w, 2], U32, name=f"quads{i}", tag=f"q{i % 4}", align_bytes=64)
             interleave(quads[i][:], planes[i][:])
 
         def finish(i):
             a, s0, w = steps[i]
             quantize(codes[a][:, s0 : s0 + w], scales[a][:, s0 : s0 + w], quads[i][:])
             if a == PASSES - 1:
-                relu = ring.tile([P, w], F32, name="relu")
+                relu = ring.tile([P, w], F32, name=f"relu{i}", tag=f"q{i % 4}", align_bytes=64)
                 for c0 in range(0, w, C):
                     e = (s0 + c0) // C
-                    acc = psum.tile([P, C], F32, name="acc", bufs=6)
-                    product(acc[:], e, codes, scales, slice(s0 + c0, s0 + c0 + C))
-                    nc.scalar.activation(relu[:, c0 : c0 + C], acc[:], ACT.Relu, bias=b_sb[:, e : e + 1])
+                    product(accs[e][:], e, codes, scales, slice(e * C, (e + 1) * C), [PASSES - 1])
+                    nc.scalar.activation(relu[:, c0 : c0 + C], accs[e][:], ACT.Relu, bias=b_sb[:, e : e + 1])
                 nc.scalar.activation(y[:, s0 : s0 + w], relu[:], ACT.Square)
+                closed[0] = (s0 + w) // C
+            if a == PASSES - 2:
+                ready[0] = (s0 + w) // C
+            while len(accs) < min(ready[0], closed[0] + BANKS):
+                e = len(accs)
+                accs.append(psum.tile([P, C], F32, name="acc", bufs=BANKS))
+                product(accs[e][:], e, codes, scales, slice(e * C, (e + 1) * C), range(PASSES - 1))
 
         side = {
             0: [lambda: cast(nc.scalar.copy, 1, 0, 0, T)],
             1: [lambda: cast(nc.scalar.copy, 1, 1, 0, T)],
-            3: [lambda: interleave(sh_quads[0][:], pairs[0][:])],
-            5: [lambda: cast(nc.scalar.copy, 2, 0, 0, T)],
-            6: [lambda: cast(nc.scalar.copy, 2, 1, 0, T)],
-            7: [lambda: interleave(sh_quads[1][:], pairs[1][:])],
-            8: [lambda: interleave(sh_quads[2][:], pairs[2][:])],
+            3: [lambda: cast(nc.scalar.copy, 2, 0, 0, T)],
+            4: [lambda: cast(nc.scalar.copy, 2, 1, 0, T)],
+            6: [lambda: interleave(sh_quads[0][:], pairs[0][:])],
+            8: [lambda: interleave(sh_quads[1][:], pairs[1][:])],
+            10: [lambda: interleave(sh_quads[2][:], pairs[2][:])],
         }
 
-        cast(nc.vector.tensor_copy, 0, 0, 0, H)
-        cast(nc.vector.tensor_copy, 0, 0, H, T)
+        for t0, t1 in HEAD:
+            cast(nc.vector.tensor_copy, 0, 0, t0, t1)
         cast(nc.scalar.copy, 0, 1, 0, T)
         for i in range(3):
             gather(i, 0)
         for i in range(len(steps)):
             if i >= 3:
                 gather(i, 0)
-            if i >= 2:
-                finish(i - 2)
+            if i >= 3:
+                finish(i - 3)
             gather(i, 1)
             weave(i)
             for work in side.get(i, []):
                 work()
-        last = len(steps) - 1
+        finish(last - 2)
         finish(last - 1)
+        first_codes = ring.tile([P, T], U32, name="first_codes", tag=plane_tag(last - 1), align_bytes=64)
+        other_codes = ring.tile([P, 2, T], U32, name="other_codes", tag=plane_tag(last), align_bytes=64)
+        sh_codes = [first_codes[:], other_codes[:, 0, :], other_codes[:, 1, :]]
         t0, w = TOKEN_PARTS[0]
         quantize(sh_codes[0][:, t0 : t0 + w], sh_scales[0][:, t0 : t0 + w], sh_quads[0][:, t0 : t0 + w, :])
         finish(last)
@@ -178,8 +186,8 @@ def tile_moe_shr_lin_relu2_kernel(
             acc = psum.tile([P, w], F32, name=f"sh_acc{part}")
             n = w if w == 512 else C
             for c0 in range(0, w, n):
-                product(acc[:, c0 : c0 + n], E, sh_codes, sh_scales, slice(t0 + c0, t0 + c0 + n))
-            relu = ring.tile([P, w], F32, name="relu")
+                product(acc[:, c0 : c0 + n], E, sh_codes, sh_scales, slice(t0 + c0, t0 + c0 + n), range(PASSES))
+            relu = keep.tile([P, w], F32, name=f"sh_relu{part}")
             nc.scalar.activation(relu[:], acc[:], ACT.Relu, bias=b_sb[:, E : E + 1])
             nc.scalar.activation(ys[:, t0 : t0 + w], relu[:], ACT.Square)
 

@@ -21,12 +21,16 @@ ALU = mybir.AluOpType
 
 STEPS = [
     (0, 0, 512), (0, 512, 512), (0, 1024, 512), (0, 1536, 512),
-    (1, 0, 512), (1, 512, 512), (0, 2048, 256), (2, 0, 512),
-    (1, 1024, 512), (2, 512, 512), (1, 1536, 512), (2, 1024, 512),
-    (1, 2048, 256), (2, 1536, 256), (2, 1792, 256), (2, 2048, 128), (2, 2176, 128),
+    (1, 0, 1024), (2, 0, 512), (2, 512, 512), (1, 1024, 1024),
+    (2, 1024, 512), (2, 1536, 512), (0, 2048, 256), (1, 2048, 256), (2, 2048, 256),
 ]
+LAG = [3, 3, 3, 3, 3, 2, 2, 2, 2, 2, 2, 3, 3]
+PLANE_SLOT = ["a", "b", "c", "a", "b", "a", "b", "a", "b", "a", "b", "d", "a"]
+QUAD_SLOT = ["d", "e", "f", "g", "d", "e", "f", "g", "d", "e", "f", "g", "b"]
+RELU_SLOT = {5: "d", 6: "e", 8: "g", 9: "e", 12: "f"}
+EMPTY_AFTER_WEAVE = {9}
 BANKS = 6
-HEAD = [(0, 512), (512, 768)]
+HEAD = [(0, 384), (384, 640), (640, 768)]
 TOKEN_PARTS = [(0, 512), (512, 256)]
 
 
@@ -41,16 +45,24 @@ def tile_moe_shr_lin_relu2_kernel(
 
         offs_sb = keep.tile([P, S // 16], U16, name="offs_sb")
         pos_sb = [keep.tile([P, T // 16], U16, name=f"pos_sb{r}") for r in range(3)]
-        raw = [[keep.tile([P, 2, T], F32, name=f"raw{a}{u}") for u in range(2)] for a in range(PASSES)]
-        pairs = [keep.tile([P, 2, T], U32, name=f"pairs{a}", align_bytes=64) for a in range(PASSES)]
+        raw = [[keep.tile([P, 2, T], F32, name=f"raw{a}{u}", tag=f"raw{a}{u}") for u in range(2)] for a in range(PASSES)]
+        pair_planes = keep.tile([P, 2 * PASSES * T], U32, name="pair_planes", align_bytes=64)
+
+        def plane_start(a, u):
+            return (2 * (PASSES - 1 - a) + u) * T
+
+        pairs = [
+            pair_planes[:, plane_start(a, 0) : plane_start(a, 0) + 2 * T].rearrange("p (u t) -> p u t", u=2)
+            for a in range(PASSES)
+        ]
         w_sb = keep.tile([P, (E + 1) * PASSES, 2 * N], U8, name="w_sb", align_bytes=64)
         ws_sb = keep.tile([P, (E + 1) * PASSES, N], U8, name="ws_sb", align_bytes=64)
         b_sb = keep.tile([P, E + 1], F32, name="b_sb")
         gate_sb = keep.tile([P, 3, T], F32, name="gate_sb")
         codes = [keep.tile([P, S], U32, name=f"codes{a}", align_bytes=64) for a in range(PASSES)]
         scales = [keep.tile([P, S], U8, name=f"scales{a}", align_bytes=64) for a in range(PASSES)]
-        sh_quads = [keep.tile([P, T, 2], U32, name=f"sh_quads{a}", align_bytes=64) for a in range(PASSES)]
-        sh_scales = [keep.tile([P, T], U8, name=f"sh_scales{a}", align_bytes=64) for a in range(PASSES)]
+        sh_quads = keep.tile([P, PASSES * T, 2], U32, name="sh_quads", align_bytes=64)
+        sh_scales = keep.tile([P, PASSES * T], U8, name="sh_scales", align_bytes=64)
         y = keep.tile([P, S], F32, name="y")
         ys = keep.tile([P, T], F32, name="ys")
         warm = keep.tile([P, 2], F32, name="warm")
@@ -109,119 +121,120 @@ def tile_moe_shr_lin_relu2_kernel(
 
         steps = STEPS
         planes, quads = {}, {}
-        accs, ready, closed = [], [0], [0]
+        accs, ready, closed = [], [0] * PASSES, [0]
 
         last = len(steps) - 1
-
-        def plane_tag(i):
-            return f"p{i % 3}"
 
         def gather(i, u):
             a, s0, w = steps[i]
             if i not in planes:
-                planes[i] = ring.tile([P, 2, w], U32, name=f"planes{i}", tag=plane_tag(i), align_bytes=64)
-            nc.vector.tensor_copy(
-                planes[i][:, u, :], pairs[a][:, u, :].indirect(offs_sb[:, s0 // 16 : (s0 + w) // 16])
-            )
+                planes[i] = ring.tile([P, 2, w], U32, name=f"planes{i}", tag=PLANE_SLOT[i], align_bytes=64)
+            start = plane_start(a, u)
+            window = pair_planes[:, start : start + (T if w < T else 2 * T)]
+            nc.vector.tensor_copy(planes[i][:, u, :], window.indirect(offs_sb[:, s0 // 16 : (s0 + w) // 16]))
 
         def weave(i):
             w = steps[i][2]
-            quads[i] = ring.tile([P, w, 2], U32, name=f"quads{i}", tag=f"q{i % 4}", align_bytes=64)
+            quads[i] = ring.tile([P, w, 2], U32, name=f"quads{i}", tag=QUAD_SLOT[i], align_bytes=64)
             interleave(quads[i][:], planes[i][:])
+
+        def open_group():
+            e = len(accs)
+            accs.append(psum.tile([P, C], F32, name="acc", bufs=BANKS))
+            product(accs[e][:], e, codes, scales, slice(e * C, (e + 1) * C), range(PASSES - 1))
+
+        def pack(i):
+            a, s0, w = steps[i]
+            quantize(codes[a][:, s0 : s0 + w], scales[a][:, s0 : s0 + w], quads[i][:])
+            ready[a] = (s0 + w) // C
 
         def finish(i):
             a, s0, w = steps[i]
-            quantize(codes[a][:, s0 : s0 + w], scales[a][:, s0 : s0 + w], quads[i][:])
             if a == PASSES - 1:
-                relu = ring.tile([P, w], F32, name=f"relu{i}", tag=f"q{i % 4}", align_bytes=64)
+                relu = ring.tile([P, w], F32, name=f"relu{i}", tag=RELU_SLOT[i], align_bytes=64)
                 for c0 in range(0, w, C):
                     e = (s0 + c0) // C
+                    if e == len(accs):
+                        open_group()
                     product(accs[e][:], e, codes, scales, slice(e * C, (e + 1) * C), [PASSES - 1])
                     nc.scalar.activation(relu[:, c0 : c0 + C], accs[e][:], ACT.Relu, bias=b_sb[:, e : e + 1])
                 nc.scalar.activation(y[:, s0 : s0 + w], relu[:], ACT.Square)
                 closed[0] = (s0 + w) // C
-            if a == PASSES - 2:
-                ready[0] = (s0 + w) // C
-            while len(accs) < min(ready[0], closed[0] + BANKS):
-                e = len(accs)
-                accs.append(psum.tile([P, C], F32, name="acc", bufs=BANKS))
-                product(accs[e][:], e, codes, scales, slice(e * C, (e + 1) * C), range(PASSES - 1))
+            while len(accs) < min(ready[0], ready[1], closed[0] + BANKS):
+                open_group()
+
+        (a0, wa), (b0, wb) = TOKEN_PARTS
+
+        def weave_shared(a):
+            if a == 0:
+                interleave(sh_quads[:, 0:wb, :], pairs[0][:, :, b0 : b0 + wb])
+                interleave(sh_quads[:, wb:T, :], pairs[0][:, :, a0 : a0 + wa])
+            else:
+                interleave(sh_quads[:, a * T : (a + 1) * T, :], pairs[a])
 
         side = {
-            0: [lambda: cast(nc.scalar.copy, 1, 0, 0, T)],
             1: [lambda: cast(nc.scalar.copy, 1, 1, 0, T)],
-            3: [lambda: cast(nc.scalar.copy, 2, 0, 0, T)],
-            4: [lambda: cast(nc.scalar.copy, 2, 1, 0, T)],
-            6: [lambda: interleave(sh_quads[0][:], pairs[0][:])],
-            8: [lambda: interleave(sh_quads[1][:], pairs[1][:])],
-            10: [lambda: interleave(sh_quads[2][:], pairs[2][:])],
+            3: [lambda: cast(nc.scalar.copy, 2, 0, 0, T), lambda: cast(nc.scalar.copy, 2, 1, 0, T)],
+            4: [lambda: weave_shared(0)],
+            5: [lambda: weave_shared(1)],
+            6: [lambda: weave_shared(2)],
         }
 
         for t0, t1 in HEAD:
             cast(nc.vector.tensor_copy, 0, 0, t0, t1)
         cast(nc.scalar.copy, 0, 1, 0, T)
+        cast(nc.scalar.copy, 1, 0, 0, T)
         for i in range(3):
             gather(i, 0)
+        done = 0
         for i in range(len(steps)):
             if i >= 3:
                 gather(i, 0)
-            if i >= 3:
-                finish(i - 3)
+            due = range(done, max(done, i - LAG[i] + 1))
+            for k in due:
+                pack(k)
+            for k in due:
+                if k not in EMPTY_AFTER_WEAVE:
+                    finish(k)
             gather(i, 1)
             weave(i)
+            for k in due:
+                if k in EMPTY_AFTER_WEAVE:
+                    finish(k)
+            done = due.stop
             for work in side.get(i, []):
                 work()
-        finish(last - 2)
-        finish(last - 1)
-        first_codes = ring.tile([P, T], U32, name="first_codes", tag=plane_tag(last - 1), align_bytes=64)
-        other_codes = ring.tile([P, 2, T], U32, name="other_codes", tag=plane_tag(last), align_bytes=64)
-        sh_codes = [first_codes[:], other_codes[:, 0, :], other_codes[:, 1, :]]
-        t0, w = TOKEN_PARTS[0]
-        quantize(sh_codes[0][:, t0 : t0 + w], sh_scales[0][:, t0 : t0 + w], sh_quads[0][:, t0 : t0 + w, :])
+        for i in range(done, last):
+            pack(i)
+            finish(i)
+        early_codes = ring.tile([P, wb], U32, name="early_codes", tag=PLANE_SLOT[last - 1], align_bytes=64)
+        quantize(early_codes[:], sh_scales[:, 0:wb], sh_quads[:, 0:wb, :])
+        pack(last)
         finish(last)
+        late_codes = ring.tile([P, PASSES * T - wb], U32, name="late_codes", tag=PLANE_SLOT[last], align_bytes=64)
+        for c0 in (0, 1024):
+            cols = slice(wb + c0, wb + c0 + 1024)
+            quantize(late_codes[:, c0 : c0 + 1024], sh_scales[:, cols], sh_quads[:, cols, :])
         for part, (t0, w) in enumerate(TOKEN_PARTS):
-            for a in range(PASSES):
-                if (part, a) != (0, 0):
-                    quantize(sh_codes[a][:, t0 : t0 + w], sh_scales[a][:, t0 : t0 + w], sh_quads[a][:, t0 : t0 + w, :])
             acc = psum.tile([P, w], F32, name=f"sh_acc{part}")
             n = w if w == 512 else C
+            starts = [wb if part == 0 else 0] + [a * T + t0 for a in range(1, PASSES)]
+            part_codes = [late_codes[:, c - wb : c - wb + w] if c else early_codes[:] for c in starts]
+            part_scales = [sh_scales[:, c : c + w] for c in starts]
             for c0 in range(0, w, n):
-                product(acc[:, c0 : c0 + n], E, sh_codes, sh_scales, slice(t0 + c0, t0 + c0 + n), range(PASSES))
+                product(acc[:, c0 : c0 + n], E, part_codes, part_scales, slice(c0, c0 + n), range(PASSES))
             relu = keep.tile([P, w], F32, name=f"sh_relu{part}")
             nc.scalar.activation(relu[:], acc[:], ACT.Relu, bias=b_sb[:, E : E + 1])
             nc.scalar.activation(ys[:, t0 : t0 + w], relu[:], ACT.Square)
 
-        terms = keep.tile([P, 3, T], F32, name="terms")
-        sums = keep.tile([P, 3, T], F32, name="sums")
-
-        def fetch(r, part):
-            t0, w = TOKEN_PARTS[part]
-            nc.vector.tensor_tensor(
-                terms[:, r, t0 : t0 + w],
-                y[:].indirect(pos_sb[r][:, t0 // 16 : (t0 + w) // 16]),
-                gate_sb[:, r, t0 : t0 + w],
-                ALU.mult,
-            )
-
-        def add(part, dst, in0, in1):
-            t0, w = TOKEN_PARTS[part]
-            nc.vector.tensor_tensor(dst[:, t0 : t0 + w], in0[:, t0 : t0 + w], in1[:, t0 : t0 + w], ALU.add)
-
-        def store(part):
-            t0, w = TOKEN_PARTS[part]
-            nc.sync.dma_start(out=out[:, t0 : t0 + w], in_=sums[:, 2, t0 : t0 + w])
-
-        fetch(0, 0)
-        fetch(1, 0)
-        fetch(2, 0)
-        add(0, sums[:, 0, :], terms[:, 0, :], terms[:, 1, :])
-        fetch(0, 1)
-        add(0, sums[:, 1, :], terms[:, 2, :], ys[:])
-        fetch(1, 1)
-        add(0, sums[:, 2, :], sums[:, 0, :], sums[:, 1, :])
-        store(0)
-        fetch(2, 1)
-        add(1, sums[:, 0, :], terms[:, 0, :], terms[:, 1, :])
-        add(1, sums[:, 1, :], terms[:, 2, :], ys[:])
-        add(1, sums[:, 2, :], sums[:, 0, :], sums[:, 1, :])
-        store(1)
+        terms = [keep.tile([P, T], F32, name=f"term{r}", tag=f"raw0{r % 2}" if r < 2 else "raw10") for r in range(3)]
+        sums = [keep.tile([P, T], F32, name=f"sum{r}", tag=("raw11", "raw20", "raw21")[r]) for r in range(3)]
+        for r in range(3):
+            nc.vector.tensor_tensor(terms[r][:], y[:].indirect(pos_sb[r][:]), gate_sb[:, r, :], ALU.mult)
+        nc.vector.tensor_tensor(sums[0][:], terms[0][:], terms[1][:], ALU.add)
+        halves = [slice(0, T // 2), slice(T // 2, T)]
+        for cols in halves:
+            nc.vector.tensor_tensor(sums[1][:, cols], terms[2][:, cols], ys[:, cols], ALU.add)
+        for cols in halves:
+            nc.vector.tensor_tensor(sums[2][:, cols], sums[0][:, cols], sums[1][:, cols], ALU.add)
+            nc.sync.dma_start(out=out[:, cols], in_=sums[2][:, cols])

@@ -21,15 +21,14 @@ ALU = mybir.AluOpType
 
 STEPS = [
     (0, 0, 512), (0, 512, 512), (0, 1024, 512), (0, 1536, 512),
-    (1, 0, 1024), (2, 0, 512), (2, 512, 512), (1, 1024, 1024),
-    (2, 1024, 512), (2, 1536, 512), (0, 2048, 256), (1, 2048, 256), (2, 2048, 256),
+    (1, 0, 1024), (2, 0, 512), (2, 512, 512), (1, 1024, 512), (2, 1024, 512),
+    (1, 1536, 512), (2, 1536, 512), (0, 2048, 256), (1, 2048, 256), (2, 2048, 256),
 ]
-LAG = [3, 3, 3, 3, 3, 2, 2, 2, 2, 2, 2, 3, 3]
-PLANE_SLOT = ["a", "b", "c", "a", "b", "a", "b", "a", "b", "a", "b", "d", "a"]
-QUAD_SLOT = ["d", "e", "f", "g", "d", "e", "f", "g", "d", "e", "f", "g", "b"]
-RELU_SLOT = {5: "d", 6: "e", 8: "g", 9: "e", 12: "f"}
-EMPTY_AFTER_WEAVE = {9}
-BANKS = 6
+LAG = [3, 3, 3, 3, 3, 3, 3, 3, 3, 3, 2, 2, 3, 3]
+PLANE_SLOT = ["a", "b", "c", "a", "b", "c", "a", "b", "c", "a", "c", "a", "e", "c"]
+QUAD_SLOT = ["d", "e", "f", "g", "d", "e", "f", "g", "d", "e", "f", "g", "d", "a"]
+RELU_SLOT = {5: "e", 6: "f", 8: "d", 10: "f", 13: "g"}
+BANKS = 8
 HEAD = [(0, 384), (384, 640), (640, 768)]
 TOKEN_PARTS = [(0, 512), (512, 256)]
 
@@ -140,7 +139,7 @@ def tile_moe_shr_lin_relu2_kernel(
 
         def open_group():
             e = len(accs)
-            accs.append(psum.tile([P, C], F32, name="acc", bufs=BANKS))
+            accs.append(psum.tile([P, C], F32, name=f"acc{e}", tag=f"bank{e % BANKS}"))
             product(accs[e][:], e, codes, scales, slice(e * C, (e + 1) * C), range(PASSES - 1))
 
         def pack(i):
@@ -193,14 +192,10 @@ def tile_moe_shr_lin_relu2_kernel(
             due = range(done, max(done, i - LAG[i] + 1))
             for k in due:
                 pack(k)
-            for k in due:
-                if k not in EMPTY_AFTER_WEAVE:
-                    finish(k)
             gather(i, 1)
             weave(i)
             for k in due:
-                if k in EMPTY_AFTER_WEAVE:
-                    finish(k)
+                finish(k)
             done = due.stop
             for work in side.get(i, []):
                 work()
@@ -216,7 +211,7 @@ def tile_moe_shr_lin_relu2_kernel(
             cols = slice(wb + c0, wb + c0 + 1024)
             quantize(late_codes[:, c0 : c0 + 1024], sh_scales[:, cols], sh_quads[:, cols, :])
         for part, (t0, w) in enumerate(TOKEN_PARTS):
-            acc = psum.tile([P, w], F32, name=f"sh_acc{part}")
+            acc = psum.tile([P, w], F32, name=f"sh_acc{part}", tag=f"bank{(E - 2 + part) % BANKS}")
             n = w if w == 512 else C
             starts = [wb if part == 0 else 0] + [a * T + t0 for a in range(1, PASSES)]
             part_codes = [late_codes[:, c - wb : c - wb + w] if c else early_codes[:] for c in starts]

@@ -29,6 +29,7 @@ PLANE_SLOT = ["a", "b", "c", "a", "b", "c", "a", "b", "c", "a", "c", "a", "e", "
 QUAD_SLOT = ["d", "e", "f", "g", "d", "e", "f", "g", "d", "e", "f", "g", "d", "a"]
 RELU_SLOT = {5: "e", 6: "f", 8: "d", 10: "f", 13: "g"}
 BANKS = 8
+SCALAR_EXPERTS = {4: 6, 9: 2}
 HEAD = [(0, 384), (384, 640), (640, 768)]
 TOKEN_PARTS = [(0, 512), (512, 256)]
 
@@ -44,7 +45,7 @@ def tile_moe_shr_lin_relu2_kernel(
 
         offs_sb = keep.tile([P, S // 16], U16, name="offs_sb")
         pos_sb = [keep.tile([P, T // 16], U16, name=f"pos_sb{r}") for r in range(3)]
-        raw = [[keep.tile([P, 2, T], F32, name=f"raw{a}{u}", tag=f"raw{a}{u}") for u in range(2)] for a in range(PASSES)]
+        raw = [[keep.tile([P, 2, T], F32, name=f"raw{a}{u}", tag=f"raw{a}{u}", align_bytes=64) for u in range(2)] for a in range(PASSES)]
         pair_planes = keep.tile([P, 2 * PASSES * T], U32, name="pair_planes", align_bytes=64)
 
         def plane_start(a, u):
@@ -58,7 +59,7 @@ def tile_moe_shr_lin_relu2_kernel(
         ws_sb = keep.tile([P, (E + 1) * PASSES, N], U8, name="ws_sb", align_bytes=64)
         b_sb = keep.tile([P, E + 1], F32, name="b_sb")
         gate_sb = keep.tile([P, 3, T], F32, name="gate_sb")
-        codes = [keep.tile([P, S], U32, name=f"codes{a}", align_bytes=64) for a in range(PASSES)]
+        singles = keep.tile([P, 2, T], BF16, name="singles", align_bytes=64)
         scales = [keep.tile([P, S], U8, name=f"scales{a}", align_bytes=64) for a in range(PASSES)]
         sh_quads = keep.tile([P, PASSES * T, 2], U32, name="sh_quads", align_bytes=64)
         sh_scales = keep.tile([P, PASSES * T], U8, name="sh_scales", align_bytes=64)
@@ -95,6 +96,9 @@ def tile_moe_shr_lin_relu2_kernel(
             dst = pairs[a][:, u, t0:t1].bitcast(BF16).rearrange("p (t j) -> p t j", j=2)
             engine_copy(dst, raw[a][u][:, :, t0:t1].rearrange("p j t -> p t j"))
 
+        def pool_copy(dst, src):
+            nc.gpsimd.tensor_scalar(dst, src, 1.0, 0.0, ALU.mult, ALU.add)
+
         def interleave(dst, src):
             nc.scalar.copy(dst.bitcast(F32), src.bitcast(F32).rearrange("p u s -> p s u"))
 
@@ -124,13 +128,27 @@ def tile_moe_shr_lin_relu2_kernel(
 
         last = len(steps) - 1
 
+        def claim(i):
+            if i not in planes:
+                planes[i] = ring.tile([P, 2, steps[i][2]], U32, name=f"planes{i}", tag=PLANE_SLOT[i], align_bytes=64)
+
+        def gather_singles(i):
+            s0, w = steps[i][1:]
+            claim(i)
+            for c0 in range(w - C * SCALAR_EXPERTS[i], w, C):
+                halves = planes[i][:, 1, c0 : c0 + C].bitcast(BF16).rearrange("p (s j) -> p s j", j=2)
+                for j in range(2):
+                    offsets = offs_sb[:, (s0 + c0) // 16 : (s0 + c0 + C) // 16]
+                    nc.scalar.activation(halves[:, :, j], singles[:, j, :].indirect(offsets), ACT.Copy)
+
         def gather(i, u):
             a, s0, w = steps[i]
-            if i not in planes:
-                planes[i] = ring.tile([P, 2, w], U32, name=f"planes{i}", tag=PLANE_SLOT[i], align_bytes=64)
+            claim(i)
+            if u == 1:
+                w -= C * SCALAR_EXPERTS.get(i, 0)
             start = plane_start(a, u)
             window = pair_planes[:, start : start + (T if w < T else 2 * T)]
-            nc.vector.tensor_copy(planes[i][:, u, :], window.indirect(offs_sb[:, s0 // 16 : (s0 + w) // 16]))
+            nc.vector.tensor_copy(planes[i][:, u, 0:w], window.indirect(offs_sb[:, s0 // 16 : (s0 + w) // 16]))
 
         def weave(i):
             w = steps[i][2]
@@ -172,17 +190,23 @@ def tile_moe_shr_lin_relu2_kernel(
                 interleave(sh_quads[:, a * T : (a + 1) * T, :], pairs[a])
 
         side = {
-            1: [lambda: cast(nc.scalar.copy, 1, 1, 0, T)],
-            3: [lambda: cast(nc.scalar.copy, 2, 0, 0, T), lambda: cast(nc.scalar.copy, 2, 1, 0, T)],
-            4: [lambda: weave_shared(0)],
-            5: [lambda: weave_shared(1)],
-            6: [lambda: weave_shared(2)],
+            0: [lambda: weave_shared(0)],
+            3: [lambda: gather_singles(4)],
+            4: [lambda: weave_shared(1)],
+            5: [lambda: weave_shared(2)],
+            7: [lambda: gather_singles(9)],
         }
 
         for t0, t1 in HEAD:
             cast(nc.vector.tensor_copy, 0, 0, t0, t1)
         cast(nc.scalar.copy, 0, 1, 0, T)
-        cast(nc.scalar.copy, 1, 0, 0, T)
+        cast(pool_copy, 1, 0, 0, T)
+        cast(pool_copy, 1, 1, 0, T)
+        pool_copy(singles[:], raw[1][1][:])
+        cast(pool_copy, 2, 0, 0, T)
+        cast(pool_copy, 2, 1, 0, T)
+        codes = [keep.tile([P, S], U32, name="codes0", tag="raw20", align_bytes=64)]
+        codes += [keep.tile([P, S], U32, name=f"codes{a}", align_bytes=64) for a in range(1, PASSES)]
         for i in range(3):
             gather(i, 0)
         done = 0
@@ -222,8 +246,8 @@ def tile_moe_shr_lin_relu2_kernel(
             nc.scalar.activation(relu[:], acc[:], ACT.Relu, bias=b_sb[:, E : E + 1])
             nc.scalar.activation(ys[:, t0 : t0 + w], relu[:], ACT.Square)
 
-        terms = [keep.tile([P, T], F32, name=f"term{r}", tag=f"raw0{r % 2}" if r < 2 else "raw10") for r in range(3)]
-        sums = [keep.tile([P, T], F32, name=f"sum{r}", tag=("raw11", "raw20", "raw21")[r]) for r in range(3)]
+        terms = [keep.tile([P, T], F32, name=f"term{r}", tag=f"raw0{r % 2}" if r < 2 else "raw10", align_bytes=64) for r in range(3)]
+        sums = [keep.tile([P, T], F32, name=f"sum{r}", tag=("raw11", "raw20", "raw21")[r], align_bytes=64) for r in range(3)]
         for r in range(3):
             nc.vector.tensor_tensor(terms[r][:], y[:].indirect(pos_sb[r][:]), gate_sb[:, r, :], ALU.mult)
         nc.vector.tensor_tensor(sums[0][:], terms[0][:], terms[1][:], ALU.add)

from contextlib import ExitStack

import concourse.mybir as mybir

K, T, E, C, N = 1536, 768, 18, 128, 128
S = E * C
P = 128
PASSES = K // 512
FLOPS = 2 * K * N * (S + T)

F32 = mybir.dt.float32
BF16 = mybir.dt.bfloat16
I32 = mybir.dt.int32
U32 = mybir.dt.uint32
U16 = mybir.dt.uint16
U8 = mybir.dt.uint8
FP8X4 = mybir.dt.float8_e4m3fn_x4
FP4X4 = mybir.dt.float4_e2m1fn_x4
ACT = mybir.ActivationFunctionType
ALU = mybir.AluOpType

STEPS = [
    (0, 0, 512), (0, 512, 512), (0, 1024, 512), (0, 1536, 512),
    (1, 0, 1024), (2, 0, 512), (2, 512, 512), (1, 1024, 512), (2, 1024, 512),
    (1, 1536, 512), (2, 1536, 512), (0, 2048, 256), (1, 2048, 256), (2, 2048, 256),
]
LAG = [3, 3, 3, 3, 3, 3, 3, 3, 3, 3, 2, 2, 3, 3]
PLANE_SLOT = ["a", "b", "c", "a", "b", "c", "a", "b", "c", "a", "c", "a", "e", "c"]
QUAD_SLOT = ["d", "e", "f", "g", "d", "e", "f", "g", "d", "e", "f", "g", "d", "a"]
RELU_SLOT = {5: "e", 6: "f", 8: "d", 10: "f", 13: "g"}
BANKS = 8
SCALAR_EXPERTS = {4: 6, 9: 2}
HEAD = [(0, 384), (384, 640), (640, 768)]
TOKEN_PARTS = [(0, 512), (512, 256)]


def tile_moe_shr_lin_relu2_kernel(
    tc, xT, w_words, w_scales, b, gate, offs, pos1, pos2, pos3, out
):
    nc = tc.nc
    with ExitStack() as ctx:
        keep = ctx.enter_context(tc.tile_pool(name="keep", bufs=1))
        ring = ctx.enter_context(tc.tile_pool(name="ring", bufs=1))
        psum = ctx.enter_context(tc.psum_pool(name="psum", bufs=1))

        offs_sb = keep.tile([P, S // 16], U16, name="offs_sb")
        pos_sb = [keep.tile([P, T // 16], U16, name=f"pos_sb{r}") for r in range(3)]
        raw = [[keep.tile([P, 2, T], F32, name=f"raw{a}{u}", tag=f"raw{a}{u}", align_bytes=64) for u in range(2)] for a in range(PASSES)]
        pair_planes = keep.tile([P, 2 * PASSES * T], U32, name="pair_planes", align_bytes=64)

        def plane_start(a, u):
            return (2 * (PASSES - 1 - a) + u) * T

        pairs = [
            pair_planes[:, plane_start(a, 0) : plane_start(a, 0) + 2 * T].rearrange("p (u t) -> p u t", u=2)
            for a in range(PASSES)
        ]
        w_sb = keep.tile([P, (E + 1) * PASSES, 2 * N], U8, name="w_sb", align_bytes=64)
        ws_sb = keep.tile([P, (E + 1) * PASSES, N], U8, name="ws_sb", align_bytes=64)
        b_sb = keep.tile([P, E + 1], F32, name="b_sb")
        gate_sb = keep.tile([P, 3, T], F32, name="gate_sb")
        singles = keep.tile([P, 2, T], BF16, name="singles", align_bytes=64)
        scales = [keep.tile([P, S], U8, name=f"scales{a}", align_bytes=64) for a in range(PASSES)]
        sh_quads = keep.tile([P, PASSES * T, 2], U32, name="sh_quads", align_bytes=64)
        sh_scales = keep.tile([P, PASSES * T], U8, name="sh_scales", align_bytes=64)
        y = keep.tile([P, S], F32, name="y")
        ys = keep.tile([P, T], F32, name="ys")
        warm = keep.tile([P, 2], F32, name="warm")

        nc.gpsimd.memset(warm[:, 0:1], 0.0)
        nc.scalar.activation(warm[:, 1:2], warm[:, 0:1], ACT.Relu)
        nc.gpsimd.memset(ws_sb[:].rearrange("p g n -> p (g n)").bitcast(I32), 0)

        def x_rows(a, u):
            return xT[512 * a : 512 * (a + 1), :].rearrange("(p j) t -> p j t", j=4)[:, 2 * u : 2 * u + 2, :]

        for t0, t1 in HEAD:
            nc.sync.dma_start(out=raw[0][0][:, :, t0:t1], in_=x_rows(0, 0)[:, :, t0:t1])
        nc.sync.dma_start(offs_sb[:], offs)
        for a in range(PASSES):
            for u in range(2):
                if (a, u) != (0, 0):
                    nc.sync.dma_start(out=raw[a][u][:], in_=x_rows(a, u))
        scale_rows = w_scales.rearrange("e a q n -> q (e a) n").bitcast(I32)
        for q in range(4):
            nc.sync.dma_start(out=ws_sb[32 * q : 32 * q + 4, :, :].bitcast(I32), in_=scale_rows[4 * q : 4 * q + 4])
        nc.sync.dma_start(out=b_sb[:], in_=b)
        word_rows = w_words.rearrange("e a p c -> p (e a) c").bitcast(I32)
        for g0, g1 in ((0, 12), (12, 24), (24, 36), (36, 57)):
            nc.sync.dma_start(out=w_sb[:, g0:g1, :].bitcast(I32), in_=word_rows[:, g0:g1, :])
        for r, pos in enumerate((pos1, pos2, pos3)):
            nc.sync.dma_start(pos_sb[r][:], pos)
        nc.sync.dma_start(out=gate_sb[:], in_=gate.rearrange("r p t -> p r t"))

        def cast(engine_copy, a, u, t0, t1):
            dst = pairs[a][:, u, t0:t1].bitcast(BF16).rearrange("p (t j) -> p t j", j=2)
            engine_copy(dst, raw[a][u][:, :, t0:t1].rearrange("p j t -> p t j"))

        def pool_copy(dst, src):
            nc.gpsimd.tensor_scalar(dst, src, 1.0, 0.0, ALU.mult, ALU.add)

        def interleave(dst, src):
            nc.scalar.copy(dst.bitcast(F32), src.bitcast(F32).rearrange("p u s -> p s u"))

        def quantize(dst_codes, dst_scales, quads):
            nc.vector.quantize_mx(
                out=dst_codes.bitcast(FP8X4),
                scales=dst_scales,
                in_=quads.rearrange("p s u -> p (s u)").bitcast(BF16),
            )

        def product(acc, e, rhs_codes, rhs_scales, cols, passes):
            for a in passes:
                g = e * PASSES + a
                nc.tensor.matmul_mx(
                    out=acc,
                    lhsT=w_sb[:, g, :].bitcast(FP4X4),
                    lhsT_scale=ws_sb[:, g, :],
                    rhs=rhs_codes[a][:, cols].bitcast(FP8X4),
                    rhs_scale=rhs_scales[a][:, cols],
                    start=(a == 0),
                    stop=(a == PASSES - 1),
                )

        steps = STEPS
        planes, quads = {}, {}
        accs, ready, closed = [], [0] * PASSES, [0]

        last = len(steps) - 1

        def claim(i):
            if i not in planes:
                planes[i] = ring.tile([P, 2, steps[i][2]], U32, name=f"planes{i}", tag=PLANE_SLOT[i], align_bytes=64)

        def gather_singles(i):
            s0, w = steps[i][1:]
            claim(i)
            for c0 in range(w - C * SCALAR_EXPERTS[i], w, C):
                halves = planes[i][:, 1, c0 : c0 + C].bitcast(BF16).rearrange("p (s j) -> p s j", j=2)
                for j in range(2):
                    offsets = offs_sb[:, (s0 + c0) // 16 : (s0 + c0 + C) // 16]
                    nc.scalar.activation(halves[:, :, j], singles[:, j, :].indirect(offsets), ACT.Copy)

        def gather(i, u):
            a, s0, w = steps[i]
            claim(i)
            if u == 1:
                w -= C * SCALAR_EXPERTS.get(i, 0)
            start = plane_start(a, u)
            window = pair_planes[:, start : start + (T if w < T else 2 * T)]
            nc.vector.tensor_copy(planes[i][:, u, 0:w], window.indirect(offs_sb[:, s0 // 16 : (s0 + w) // 16]))

        def weave(i):
            w = steps[i][2]
            quads[i] = ring.tile([P, w, 2], U32, name=f"quads{i}", tag=QUAD_SLOT[i], align_bytes=64)
            interleave(quads[i][:], planes[i][:])

        def open_group():
            e = len(accs)
            accs.append(psum.tile([P, C], F32, name=f"acc{e}", tag=f"bank{e % BANKS}"))
            product(accs[e][:], e, codes, scales, slice(e * C, (e + 1) * C), range(PASSES - 1))

        def pack(i):
            a, s0, w = steps[i]
            quantize(codes[a][:, s0 : s0 + w], scales[a][:, s0 : s0 + w], quads[i][:])
            ready[a] = (s0 + w) // C

        def finish(i):
            a, s0, w = steps[i]
            if a == PASSES - 1:
                relu = ring.tile([P, w], F32, name=f"relu{i}", tag=RELU_SLOT[i], align_bytes=64)
                for c0 in range(0, w, C):
                    e = (s0 + c0) // C
                    if e == len(accs):
                        open_group()
                    product(accs[e][:], e, codes, scales, slice(e * C, (e + 1) * C), [PASSES - 1])
                    nc.scalar.activation(relu[:, c0 : c0 + C], accs[e][:], ACT.Relu, bias=b_sb[:, e : e + 1])
                nc.scalar.activation(y[:, s0 : s0 + w], relu[:], ACT.Square)
                closed[0] = (s0 + w) // C
            while len(accs) < min(ready[0], ready[1], closed[0] + BANKS):
                open_group()

        (a0, wa), (b0, wb) = TOKEN_PARTS

        def weave_shared(a):
            if a == 0:
                interleave(sh_quads[:, 0:wb, :], pairs[0][:, :, b0 : b0 + wb])
                interleave(sh_quads[:, wb:T, :], pairs[0][:, :, a0 : a0 + wa])
            else:
                interleave(sh_quads[:, a * T : (a + 1) * T, :], pairs[a])

        side = {
            0: [lambda: weave_shared(0)],
            3: [lambda: gather_singles(4)],
            4: [lambda: weave_shared(1)],
            5: [lambda: weave_shared(2)],
            7: [lambda: gather_singles(9)],
        }

        for t0, t1 in HEAD:
            cast(nc.vector.tensor_copy, 0, 0, t0, t1)
        cast(nc.scalar.copy, 0, 1, 0, T)
        cast(pool_copy, 1, 0, 0, T)
        cast(pool_copy, 1, 1, 0, T)
        pool_copy(singles[:], raw[1][1][:])
        cast(pool_copy, 2, 0, 0, T)
        cast(pool_copy, 2, 1, 0, T)
        codes = [keep.tile([P, S], U32, name="codes0", tag="raw20", align_bytes=64)]
        codes += [keep.tile([P, S], U32, name=f"codes{a}", align_bytes=64) for a in range(1, PASSES)]
        for i in range(3):
            gather(i, 0)
        done = 0
        for i in range(len(steps)):
            if i >= 3:
                gather(i, 0)
            due = range(done, max(done, i - LAG[i] + 1))
            for k in due:
                pack(k)
            gather(i, 1)
            weave(i)
            for k in due:
                finish(k)
            done = due.stop
            for work in side.get(i, []):
                work()
        for i in range(done, last):
            pack(i)
            finish(i)
        early_codes = ring.tile([P, wb], U32, name="early_codes", tag=PLANE_SLOT[last - 1], align_bytes=64)
        quantize(early_codes[:], sh_scales[:, 0:wb], sh_quads[:, 0:wb, :])
        pack(last)
        finish(last)
        late_codes = ring.tile([P, PASSES * T - wb], U32, name="late_codes", tag=PLANE_SLOT[last], align_bytes=64)
        for c0 in (0, 1024):
            cols = slice(wb + c0, wb + c0 + 1024)
            quantize(late_codes[:, c0 : c0 + 1024], sh_scales[:, cols], sh_quads[:, cols, :])
        for part, (t0, w) in enumerate(TOKEN_PARTS):
            acc = psum.tile([P, w], F32, name=f"sh_acc{part}", tag=f"bank{(E - 2 + part) % BANKS}")
            n = w if w == 512 else C
            starts = [wb if part == 0 else 0] + [a * T + t0 for a in range(1, PASSES)]
            part_codes = [late_codes[:, c - wb : c - wb + w] if c else early_codes[:] for c in starts]
            part_scales = [sh_scales[:, c : c + w] for c in starts]
            for c0 in range(0, w, n):
                product(acc[:, c0 : c0 + n], E, part_codes, part_scales, slice(c0, c0 + n), range(PASSES))
            relu = keep.tile([P, w], F32, name=f"sh_relu{part}")
            nc.scalar.activation(relu[:], acc[:], ACT.Relu, bias=b_sb[:, E : E + 1])
            nc.scalar.activation(ys[:, t0 : t0 + w], relu[:], ACT.Square)

        terms = [keep.tile([P, T], F32, name=f"term{r}", tag=f"raw0{r % 2}" if r < 2 else "raw10", align_bytes=64) for r in range(3)]
        sums = [keep.tile([P, T], F32, name=f"sum{r}", tag=("raw11", "raw20", "raw21")[r], align_bytes=64) for r in range(3)]
        for r in range(3):
            nc.vector.tensor_tensor(terms[r][:], y[:].indirect(pos_sb[r][:]), gate_sb[:, r, :], ALU.mult)
        nc.vector.tensor_tensor(sums[0][:], terms[0][:], terms[1][:], ALU.add)
        halves = [slice(0, T // 2), slice(T // 2, T)]
        for cols in halves:
            nc.vector.tensor_tensor(sums[1][:, cols], terms[2][:, cols], ys[:, cols], ALU.add)
        for cols in halves:
            nc.vector.tensor_tensor(sums[2][:, cols], sums[0][:, cols], sums[1][:, cols], ALU.add)
            nc.sync.dma_start(out=out[:, cols], in_=sums[2][:, cols])
